import numpy as np
import ml_dtypes

BF16 = ml_dtypes.bfloat16


def bf(x):
    return np.asarray(x, np.float32).astype(BF16)


def f32(x):
    return np.asarray(x, np.float32)


def f64(x):
    return np.asarray(x).astype(np.float64)


def striped(idx):
    return np.concatenate([l.reshape(-1, 16).T for l in idx])


def rows(idx, k):
    return np.tile(np.repeat(idx, 16, axis=0), (k // (16 * 8), 1))


def look(tab, idx):
    return np.take_along_axis(f64(tab), rows(idx, len(tab)), axis=1)


K, S, D, V, N, M = 128, 2048, 2, 512, 1024, 256


def setup_inputs():
    return {"tab": f32(np.random.standard_normal((K, S))), "u0": f32(np.random.uniform(0.2, 1.0, (K, V))), "u1": f32(np.random.uniform(0.2, 1.0, (K, V))), "w": bf(np.random.standard_normal((K, M)) / np.sqrt(K)), "b": f32(0.5 * np.random.standard_normal((M, 1))), "offs": striped(np.stack([np.random.permutation(S)[:N] for _ in range(8)]))}


def reference(tab, u0, u1, w, b, offs):
    idx = np.stack([g.T.reshape(-1) for g in np.split(offs, 8)])
    x = f64(u0) * np.minimum(np.maximum(look(tab, idx[:, :V]), -1.25), 1.0) + f64(u1) * np.minimum(np.maximum(look(tab, idx[:, 1 * V:2 * V]), -1.25), 1.0)
    return np.maximum(f64(w).T @ x + f64(b), 0.0)

@@ -1,0 +1,68 @@
+import concourse.mybir as mybir
+
+F32, BF16, U16 = mybir.dt.float32, mybir.dt.bfloat16, mybir.dt.uint16
+MULT, ADD = mybir.AluOpType.mult, mybir.AluOpType.add
+MAX, MIN = mybir.AluOpType.max, mybir.AluOpType.min
+RELU = mybir.ActivationFunctionType.Relu
+
+P = 128
+S = 2048
+V = 512
+D = 2
+M = 256
+LOW, HIGH = -1.25, 1.0
+
+LIST_COLUMNS = V // 16
+HALF = V // 2
+
+FLOPS = 2 * P * M * V
+
+
+def tile_lookup_clipmix_relu_kernel(tc, tab, u0, u1, w, b, offs, out):
+    nc = tc.nc
+    with (
+        tc.tile_pool(name="held", bufs=1) as held,
+        tc.tile_pool(name="results", bufs=4) as results,
+        tc.psum_pool(name="psum", bufs=4) as psum,
+    ):
+        offsets = held.tile([P, D * LIST_COLUMNS], U16, name="offsets")
+        table = held.tile([P, S], F32, name="table")
+        weights = [held.tile([P, V], F32, name=f"weights{d}") for d in range(D)]
+        matrix = held.tile([P, M], BF16, name="matrix")
+        biases = [held.tile([P, 1], F32, name=f"bias{m}") for m in range(M // P)]
+
+        nc.sync.dma_start(offsets[:], offs)
+        nc.sync.dma_start(table[:, : S // 2], tab[:, : S // 2])
+        nc.scalar.dma_start(table[:, S // 2 :], tab[:, S // 2 :])
+        nc.sync.dma_start(weights[0][:], u0)
+        nc.scalar.dma_start(weights[1][:], u1)
+        nc.gpsimd.dma_start(matrix[:], w)
+        for m in range(M // P):
+            nc.gpsimd.dma_start(biases[m][:], b[m * P : (m + 1) * P, :])
+
+        def clamped_look_up(d):
+            picked = held.tile([P, V], F32, name=f"picked{d}")
+            entries = offsets[:, d * LIST_COLUMNS : (d + 1) * LIST_COLUMNS]
+            nc.vector.tensor_scalar(picked[:], table[:].indirect(entries), LOW, HIGH, MAX, MIN)
+            return picked
+
+        picked0 = clamped_look_up(0)
+        product0 = held.tile([P, V], F32, name="product0")
+        nc.vector.tensor_tensor(product0[:], picked0[:], weights[0][:], MULT)
+        picked1 = clamped_look_up(1)
+
+        product1 = held.tile([P, V], F32, name="product1")
+        x = held.tile([P, V], BF16, name="x")
+        for half in range(2):
+            columns = slice(half * HALF, (half + 1) * HALF)
+            nc.vector.tensor_tensor(product1[:, columns], picked1[:, columns], weights[1][:, columns], MULT)
+            nc.vector.tensor_tensor(x[:, columns], product0[:, columns], product1[:, columns], ADD)
+            for m in range(M // P):
+                sums = psum.tile([P, HALF], F32, name="sums")
+                nc.tensor.matmul(sums[:], matrix[:, m * P : (m + 1) * P], x[:, columns], start=True, stop=True)
+                result = results.tile([P, HALF], F32, name="result")
+                if m == 0:
+                    nc.scalar.activation(result[:], sums[:], RELU, bias=biases[m][:])
+                else:
+                    nc.vector.tensor_scalar(result[:], sums[:], biases[m][:], 0.0, ADD, MAX)
+                nc.sync.dma_start(out[m * P : (m + 1) * P, columns], result[:])

@@ -31,38 +31,36 @@ def tile_lookup_clipmix_relu_kernel(tc, tab, u0, u1, w, b, offs, out):
         matrix = held.tile([P, M], BF16, name="matrix")
         biases = [held.tile([P, 1], F32, name=f"bias{m}") for m in range(M // P)]
 
-        nc.sync.dma_start(offsets[:], offs)
         nc.sync.dma_start(table[:, : S // 2], tab[:, : S // 2])
         nc.scalar.dma_start(table[:, S // 2 :], tab[:, S // 2 :])
+        nc.sync.dma_start(offsets[:], offs)
         nc.sync.dma_start(weights[0][:], u0)
         nc.scalar.dma_start(weights[1][:], u1)
-        nc.gpsimd.dma_start(matrix[:], w)
+        nc.sync.dma_start(matrix[:], w)
         for m in range(M // P):
-            nc.gpsimd.dma_start(biases[m][:], b[m * P : (m + 1) * P, :])
+            nc.scalar.dma_start(biases[m][:], b[m * P : (m + 1) * P, :])
 
-        def clamped_look_up(d):
-            picked = held.tile([P, V], F32, name=f"picked{d}")
+        picked = [held.tile([P, V], F32, name=f"picked{d}") for d in range(D)]
+        for d in range(D):
             entries = offsets[:, d * LIST_COLUMNS : (d + 1) * LIST_COLUMNS]
-            nc.vector.tensor_scalar(picked[:], table[:].indirect(entries), LOW, HIGH, MAX, MIN)
-            return picked
+            nc.vector.tensor_scalar(picked[d][:], table[:].indirect(entries), LOW, HIGH, MAX, MIN)
 
-        picked0 = clamped_look_up(0)
-        product0 = held.tile([P, V], F32, name="product0")
-        nc.vector.tensor_tensor(product0[:], picked0[:], weights[0][:], MULT)
-        picked1 = clamped_look_up(1)
-
-        product1 = held.tile([P, V], F32, name="product1")
+        halves = [slice(half * HALF, (half + 1) * HALF) for half in range(2)]
+        products = [held.tile([P, V], F32, name=f"product{d}") for d in range(D)]
         x = held.tile([P, V], BF16, name="x")
-        for half in range(2):
-            columns = slice(half * HALF, (half + 1) * HALF)
-            nc.vector.tensor_tensor(product1[:, columns], picked1[:, columns], weights[1][:, columns], MULT)
-            nc.vector.tensor_tensor(x[:, columns], product0[:, columns], product1[:, columns], ADD)
+        nc.vector.tensor_tensor(products[0][:], picked[0][:], weights[0][:], MULT)
+        for columns in halves:
+            nc.vector.tensor_tensor(products[1][:, columns], picked[1][:, columns], weights[1][:, columns], MULT)
+        for columns in halves:
+            nc.vector.tensor_tensor(x[:, columns], products[0][:, columns], products[1][:, columns], ADD)
+
+        for half, columns in enumerate(halves):
             for m in range(M // P):
                 sums = psum.tile([P, HALF], F32, name="sums")
                 nc.tensor.matmul(sums[:], matrix[:, m * P : (m + 1) * P], x[:, columns], start=True, stop=True)
                 result = results.tile([P, HALF], F32, name="result")
-                if m == 0:
-                    nc.scalar.activation(result[:], sums[:], RELU, bias=biases[m][:])
-                else:
+                if half == 1 and m == M // P - 1:
                     nc.vector.tensor_scalar(result[:], sums[:], biases[m][:], 0.0, ADD, MAX)
+                else:
+                    nc.scalar.activation(result[:], sums[:], RELU, bias=biases[m][:])
                 nc.sync.dma_start(out[m * P : (m + 1) * P, columns], result[:])

@@ -15,6 +15,8 @@ LOW, HIGH = -1.25, 1.0
 LIST_COLUMNS = V // 16
 HALF = V // 2
 
+WARM_UP = 3
+
 FLOPS = 2 * P * M * V
 
 
@@ -40,6 +42,10 @@ def tile_lookup_clipmix_relu_kernel(tc, tab, u0, u1, w, b, offs, out):
         for m in range(M // P):
             nc.scalar.dma_start(biases[m][:], b[m * P : (m + 1) * P, :])
 
+        warm = psum.tile([P, HALF], F32, name="warm")
+        for i in range(WARM_UP):
+            nc.tensor.matmul(warm[:], table[:, :P], table[:, S - HALF :], start=i == 0, stop=i == WARM_UP - 1)
+
         picked = [held.tile([P, V], F32, name=f"picked{d}") for d in range(D)]
         for d in range(D):
             entries = offsets[:, d * LIST_COLUMNS : (d + 1) * LIST_COLUMNS]
@@ -54,13 +60,14 @@ def tile_lookup_clipmix_relu_kernel(tc, tab, u0, u1, w, b, offs, out):
         for columns in halves:
             nc.vector.tensor_tensor(x[:, columns], products[0][:, columns], products[1][:, columns], ADD)
 
-        for half, columns in enumerate(halves):
+        for columns in halves:
             for m in range(M // P):
                 sums = psum.tile([P, HALF], F32, name="sums")
                 nc.tensor.matmul(sums[:], matrix[:, m * P : (m + 1) * P], x[:, columns], start=True, stop=True)
                 result = results.tile([P, HALF], F32, name="result")
-                if half == 1 and m == M // P - 1:
-                    nc.vector.tensor_scalar(result[:], sums[:], biases[m][:], 0.0, ADD, MAX)
-                else:
+                if m % 2 == 0:
                     nc.scalar.activation(result[:], sums[:], RELU, bias=biases[m][:])
-                nc.sync.dma_start(out[m * P : (m + 1) * P, columns], result[:])
+                    nc.scalar.dma_start(out[m * P : (m + 1) * P, columns], result[:])
+                else:
+                    nc.vector.tensor_scalar(result[:], sums[:], biases[m][:], 0.0, ADD, MAX)
+                    nc.sync.dma_start(out[m * P : (m + 1) * P, columns], result[:])

import concourse.mybir as mybir

F32, BF16, U16 = mybir.dt.float32, mybir.dt.bfloat16, mybir.dt.uint16
MULT, ADD = mybir.AluOpType.mult, mybir.AluOpType.add
MAX, MIN = mybir.AluOpType.max, mybir.AluOpType.min
RELU = mybir.ActivationFunctionType.Relu

P = 128
S = 2048
V = 512
D = 2
M = 256
LOW, HIGH = -1.25, 1.0

LIST_COLUMNS = V // 16
HALF = V // 2

WARM_UP = 3

FLOPS = 2 * P * M * V


def tile_lookup_clipmix_relu_kernel(tc, tab, u0, u1, w, b, offs, out):
    nc = tc.nc
    with (
        tc.tile_pool(name="held", bufs=1) as held,
        tc.tile_pool(name="results", bufs=4) as results,
        tc.psum_pool(name="psum", bufs=4) as psum,
    ):
        offsets = held.tile([P, D * LIST_COLUMNS], U16, name="offsets")
        table = held.tile([P, S], F32, name="table")
        weights = [held.tile([P, V], F32, name=f"weights{d}") for d in range(D)]
        matrix = held.tile([P, M], BF16, name="matrix")
        biases = [held.tile([P, 1], F32, name=f"bias{m}") for m in range(M // P)]

        nc.sync.dma_start(table[:, : S // 2], tab[:, : S // 2])
        nc.scalar.dma_start(table[:, S // 2 :], tab[:, S // 2 :])
        nc.sync.dma_start(offsets[:], offs)
        nc.sync.dma_start(weights[0][:], u0)
        nc.scalar.dma_start(weights[1][:], u1)
        nc.sync.dma_start(matrix[:], w)
        for m in range(M // P):
            nc.scalar.dma_start(biases[m][:], b[m * P : (m + 1) * P, :])

        warm = psum.tile([P, HALF], F32, name="warm")
        for i in range(WARM_UP):
            nc.tensor.matmul(warm[:], table[:, :P], table[:, S - HALF :], start=i == 0, stop=i == WARM_UP - 1)

        picked = [held.tile([P, V], F32, name=f"picked{d}") for d in range(D)]
        for d in range(D):
            entries = offsets[:, d * LIST_COLUMNS : (d + 1) * LIST_COLUMNS]
            nc.vector.tensor_scalar(picked[d][:], table[:].indirect(entries), LOW, HIGH, MAX, MIN)

        halves = [slice(half * HALF, (half + 1) * HALF) for half in range(2)]
        products = [held.tile([P, V], F32, name=f"product{d}") for d in range(D)]
        x = held.tile([P, V], BF16, name="x")
        nc.vector.tensor_tensor(products[0][:], picked[0][:], weights[0][:], MULT)
        for columns in halves:
            nc.vector.tensor_tensor(products[1][:, columns], picked[1][:, columns], weights[1][:, columns], MULT)
        for columns in halves:
            nc.vector.tensor_tensor(x[:, columns], products[0][:, columns], products[1][:, columns], ADD)

        for columns in halves:
            for m in range(M // P):
                sums = psum.tile([P, HALF], F32, name="sums")
                nc.tensor.matmul(sums[:], matrix[:, m * P : (m + 1) * P], x[:, columns], start=True, stop=True)
                result = results.tile([P, HALF], F32, name="result")
                if m % 2 == 0:
                    nc.scalar.activation(result[:], sums[:], RELU, bias=biases[m][:])
                    nc.scalar.dma_start(out[m * P : (m + 1) * P, columns], result[:])
                else:
                    nc.vector.tensor_scalar(result[:], sums[:], biases[m][:], 0.0, ADD, MAX)
                    nc.sync.dma_start(out[m * P : (m + 1) * P, columns], result[:])
